import numpy as np
CORES = [6,14,22,30,38,134,142,150,158]
N = 9
T, FF, CAP, CAPP = 4096, 4, 1152, 256
def entries(a): return a.T.reshape(-1)
def pack(v, P): return np.ascontiguousarray(np.asarray(v, np.int32).reshape(-1, P).T)
def lists(rng, how):
    O = np.stack([rng.permutation(np.repeat(np.arange(N), CAPP))[:CAP] for k in range(N)])
    if how == "apart": s = int(rng.integers(N * CAPP - CAP + 1)); cnt = np.bincount(np.repeat(np.arange(N), CAPP)[s:s + CAP], minlength=N); a = rng.permutation(N); O = np.stack([rng.permutation(np.repeat(np.arange(N), cnt[(a + k) % N])) for k in rng.permutation(N)])
    if how == "full": z = rng.permutation(N); O = np.stack([rng.permutation(np.repeat(z, CAPP)[:CAP]) for k in range(N)])
    if how == "none": z = int(rng.integers(N)); O = np.stack([rng.permutation(np.repeat(np.delete(np.arange(N), z), CAPP))[:CAP] for k in range(N)])
    P = np.zeros((N, CAP), np.int64)
    for o in range(N):
        q = rng.permutation(T); u = 0
        for k in range(N):
            m = np.nonzero(O[k] == o)[0]
            if how != "apart": q = rng.permutation(T); u = 0
            if how == "sorted": q = np.r_[0, T - 1, 1 + rng.permutation(T - 2)]
            P[k, m] = T * o + q[u:u + len(m)]; u += len(m)
    if how == "same": P = np.stack([rng.permutation(P[0]) for k in range(N)])
    if how == "sorted": P = np.sort(P, axis=1)
    G = 2 * rng.random((N, 16, CAP // 16), dtype=np.float32) - 1
    if how == "none": G[rng.random(G.shape) < 0.125] = 0
    return {"gate": G, "pick": np.stack([pack(p, 16) for p in P])}
def setup_inputs(rng):
    return dict({"x": rng.standard_normal((N, 128, T), dtype=np.float32), "w1": (rng.standard_normal((N, 128, FF * 128), dtype=np.float32) / 8), "w2": (rng.standard_normal((N, 128, FF * 128), dtype=np.float32) / 16)}, **lists(rng, "uniform"))
def setup_inputs_apart(rng):
    d = setup_inputs(rng); d.update(lists(rng, "apart"))
    for k in ("x",): d[k] = (d[k].astype(np.float32) * 1024.0).astype(d[k].dtype)
    return d
def setup_inputs_full(rng):
    d = setup_inputs(rng); d.update(lists(rng, "full"))
    for k in ("x",): d[k] = (d[k].astype(np.float32) * (1 / 1024.0)).astype(d[k].dtype)
    return d
def setup_inputs_none(rng):
    d = setup_inputs(rng); d.update(lists(rng, "none"))
    return d
def setup_inputs_same(rng):
    d = setup_inputs(rng); d.update(lists(rng, "same"))
    return d
def setup_inputs_sorted(rng):
    d = setup_inputs(rng); d.update(lists(rng, "sorted"))
    return d
def check_inputs(x):
    bad = []
    if x["pick"].min() < 0 or x["pick"].max() >= N * T: bad.append("pick out of range")
    if any(len(np.unique(a)) != a.size for a in x["pick"]): bad.append("a token stands twice in a list")
    if max(int(np.bincount(entries(a) // T, minlength=N).max()) for a in x["pick"]) > CAPP: bad.append("more than CAPP of an expert's tokens lie on one rank")
    return bad
def reference(x, w1, w2, gate, pick):
    X, W1, W2 = x.astype(np.float64), w1.astype(np.float64), w2.astype(np.float64)
    A = np.concatenate(list(X), axis=1); Y = np.zeros((128, N * T))
    for k in range(N):
        P = entries(pick[k]); g = entries(gate[k]).astype(np.float64)
        Y[:, P] += g[None, :] * sum(W2[k][:, 128 * f:128 * f + 128].T @ np.maximum(W1[k][:, 128 * f:128 * f + 128].T @ A[:, P], 0.0) for f in range(FF))
    return {"y": np.stack([Y[:, T * r:T * r + T] for r in range(N)]).astype(np.float32)}

from concourse.bass import DstId, RemoteDMATransfer
from concourse.mybir import dt, AluOpType, ActivationFunctionType

N, TK = 9, 4096
OP = AluOpType
AF = ActivationFunctionType

SCRATCH = {
    "xs": ("sbuf", [128, 4100], "float32"),
    "yb": ("sbuf", [128, 4356], "float32"),
    "W": ("sbuf", [128, 1024], "float32"),
    "gx": ("sbuf", [128, 9 * 256], "float32"),
    "res": ("sbuf", [128, 8 * 256], "float32"),
    "rl": ("sbuf", [128, 512], "float32"),
    "tok": ("sbuf", [128, 256], "float32"),
    "hs": ("sbuf", [128, 1024], "float32"),
    "ro": ("sbuf", [128, 256], "float32"),
    "Gb": ("sbuf", [128, 256], "float32"),
    "tmp": ("sbuf", [128, 512], "float32"),
    "grow": ("sbuf", [1, 512], "float32"),
    "onesf": ("sbuf", [128, 128], "float32"),
    "pk": ("sbuf", [128, 9], "int32"),
    "gt": ("sbuf", [128, 9], "float32"),
    "ow": ("sbuf", [128, 9], "int32"),
    "loc": ("sbuf", [128, 9], "int32"),
    "ge": ("sbuf", [128, 9], "float32"),
    "df": ("sbuf", [128, 9], "float32"),
    "cci": ("sbuf", [128, 9], "int32"),
    "cc16": ("sbuf", [128, 9], "float32"),
    "ci": ("sbuf", [128, 16], "int32"),
    "cidx": ("sbuf", [128, 16], "uint16"),
    "pi": ("sbuf", [128, 1], "int32"),
    "pm": ("sbuf", [128, 1], "int32"),
    "pf": ("sbuf", [128, 1], "float32"),
    "oc": ("sbuf", [128, 144], "float32"),
    "rm": ("sbuf", [128, 144], "float32"),
    "ub": ("sbuf", [128, 144], "float32"),
    "sc": ("sbuf", [128, 144], "float32"),
    "m16": ("sbuf", [128, 128], "bfloat16"),
    "st16": ("sbuf", [128, 144], "bfloat16"),
    "ones": ("sbuf", [128, 128], "bfloat16"),
    "nb": ("sbuf", [128, 128], "bfloat16"),
    "U": ("sbuf", [128, 128], "bfloat16"),
    "nI": ("sbuf", [128, 128], "bfloat16"),
    "rowc": ("sbuf", [128, 144], "bfloat16"),
    "E": ("sbuf", [128, 144], "bfloat16"),
    "LQ": ("sbuf", [128, 9 * 128], "float16"),
    "RC": ("sbuf", [128, 9 * 144], "float16"),
    "GA": ("sbuf", [128, 9 * 144], "float32"),
    "GQ": ("sbuf", [128, 9 * 16], "float32"),
    "gs1": ("sbuf", [128, 16], "float32"),
    "gs2": ("sbuf", [128, 16], "float32"),
    "L16": ("sbuf", [128, 144], "uint16"),
    "Lt": ("sbuf", [128, 144], "uint16"),
    "L2": ("sbuf", [128, 144], "uint16"),
    "lf": ("sbuf", [128, 144], "float32"),
    "lm": ("sbuf", [128, 144], "float32"),
    "gd": ("dram", [9, 128, 2], "float32"),
    "gl": ("dram", [2, 128, 2], "float32"),
    "psP": ("psum", [128, 512], "float32"),
    "psL": ("psum", [128, 512], "float32"),
    "psG": ("psum", [128, 512], "float32"),
    "po": ("psum", [128, 512], "float32"),
    "h0": ("psum", [128, 512], "float32"),
    "h1": ("psum", [128, 512], "float32"),
    "h2": ("psum", [128, 512], "float32"),
    "h3": ("psum", [128, 512], "float32"),
}
SEMAPHORES = (["v", "a", "p", "gi", "dp", "dgt", "dw", "dx", "dgs", "dgr", "dy", "ls", "wh", "wa", "ta0", "ta1",
               "ga0", "ga1", "dg0", "dg1", "rl0", "rl1"] + ["l%d" % c for c in range(8)] + ["ra%d" % c for c in range(8)])

_cache = {}
ROLE = "bcabcarr"


def colour(o, k):
    return (k - o - 1) % N


def plan(cores, topo):
    if "plan" in _cache:
        return _cache["plan"]
    allc = list(range(256))
    where = {c: (topo.host(c), topo.chip(c)) for c in allc}
    chips = {}
    for c in allc:
        chips.setdefault(where[c], []).append(c)
    taken = {where[c] for c in cores}
    P = {"jobs": {}, "dest": {}, "site": {}, "foreign": [], "local": [], "porters": [], "plain": [], "relay": []}

    def same(a, b):
        return where[a] == where[b] or topo.same_plane(a, b)

    for prefer in (True, False):
        for k, R in enumerate(cores):
            if prefer:
                P["foreign"].append(None)
            if P["foreign"][k] is not None:
                continue
            for ch in sorted(chips):
                c0 = chips[ch][0]
                if ch in taken or same(R, c0) or (prefer and not topo.mates(R, c0)):
                    continue
                P["foreign"][k] = list(chips[ch])
                taken.add(ch)
                break
    for k, R in enumerate(cores):
        loc = [c for c in chips[where[R]] if c != R]
        other = P["foreign"][k][0]
        por = [c for c in loc if topo.may_write(c, other)]
        P["local"].append(loc)
        P["porters"].append(por)
        P["plain"].append([c for c in loc if c not in por])
        far = [c for c in por if topo.die(c) != topo.die(R)]
        near = [c for c in por if topo.die(c) == topo.die(R)]
        P["relay"].append({"a": near[0], "b": far[0], "c": far[1], "r": R})
        src = [o for o in range(N) if o != k]
        home = [o for o in src if same(cores[o], R)]
        away = [o for o in src if o not in home]
        if len(away) > 4:
            m = [o for o in away if topo.mates(cores[o], R)][0]
            away.remove(m)
            home.append(m)
        for srcs, site in ((home, loc), (away, P["foreign"][k])):
            for half, d in ((0, topo.die(R)), (1, 1 - topo.die(R))):
                free = [c for c in site if topo.die(c) == d]
                todo = sorted(srcs, key=lambda o: colour(o, k))
                need = [o for o in todo if not all(topo.may_write(c, cores[o]) for c in free)]
                got = []
                for o in need:
                    c = [c for c in free if topo.may_write(c, cores[o])][-1]
                    got.append((o, c))
                    free.remove(c)
                    todo.remove(o)
                if len(todo) > len(free):
                    c = free.pop(0)
                    got += [(todo[0], c), (todo[-1], c)]
                    todo = todo[1:-1]
                got += list(zip(todo, free))
                for o, c in got:
                    slot = len(P["jobs"].setdefault(c, []))
                    P["jobs"][c].append((k, o, half))
                    P["dest"][(k, o, half)] = (c, slot)
        for c in loc + P["foreign"][k]:
            P["site"][c] = k
    _cache["plan"] = P
    return P


def rank_program(g, core, T, topo):
    P = plan(T.cores, topo)
    r = T.rank_of(core)
    S = T.sem
    if r is None and core not in P["site"]:
        return
    n = {"v": 0, "a": 0, "p": 0, "gi": 0, "ls": 0}

    def tick(q, ins):
        ins.then_inc(S[q], 1)
        n[q] += 1
        return n[q]

    def parts(dst, cnt, width):
        m = topo.mask(core, dst)
        b = [i for i in range(16) if (m >> i) & 1]
        return [sum(1 << e for e in b[i * width:(i + 1) * width]) for i in range(cnt)]

    def send(items):
        tr = []
        for dsts, out, src, sem, mask in items:
            ids = []
            for d in dsts:
                rid, pid = topo.addr(d, core)
                ids.append(DstId(rid=rid, pnc=pid))
            tr.append(RemoteDMATransfer(dst_ids=ids, dma_engine_mask=mask, remote_sem=sem, srcs=[src],
                                        dsts=[out] * len(ids)))
            n["ls"] += bin(mask).count("1")
        g.remote_dma_fused(tr, local_sem=S.ls)

    def dispatch(k, o, buf, col):
        it = []
        d0 = P["dest"][(k, o, 0)][0]
        ms = parts(d0, 2, 4)
        for h in (0, 1):
            d, slot = P["dest"][(k, o, h)]
            it.append(([d], T.tok[:, 128 * slot:128 * slot + 128], buf[:, col + 128 * h:col + 128 * h + 128],
                       S["ta%d" % slot], ms[h]))
        send(it)

    V, A, PE = g.vector, g.scalar, g.tensor
    HB = [T.h0, T.h1, T.h2, T.h3]

    def vw(q, val):
        V.wait_ge(S[q], val)

    if r is None:
        k = P["site"][core]
        R = T.cores[k]
        jobs = P["jobs"].get(core, [])
        tick("v", V.memset(T.onesf[:], 1.0))
        loc, fo, por, plain = P["local"][k], P["foreign"][k], P["porters"][k], P["plain"][k]
        g.wait_ge(S.wh, 4)
        if core in loc:
            others = [c for c in loc if c != core]
            if core in por:
                i = por.index(core)
                a, w = 256 * i, 256
                ms = parts(fo[0], 2, 4)
                send([([fo[2 * i + j]], T.W[:, a + 128 * j:a + 128 * j + 128], T.W[:, a + 128 * j:a + 128 * j + 128],
                       S.wh, ms[j]) for j in (0, 1)])
            else:
                a, w = 768 + 64 * plain.index(core), 64
        else:
            others = [c for c in fo if c != core]
            a, w = 128 * fo.index(core), 128
        send([(others, T.W[:, a:a + w], T.W[:, a:a + w], S.wa, parts(others[0], 1, 16)[0])])
        nwa = 16 * len(others)
        if core in loc:
            me = [x for x in "abc" if P["relay"][k][x] == core]
            if me:
                mine = [c for c in range(8) if ROLE[c] == me[0]]
                for s, c in enumerate(mine):
                    g.wait_ge(S["rl%d" % s], 8)
                    dispatch((k + 1 + c) % N, k, T.rl, 256 * s)
        OB, GBK = [T.po, T.psP], [T.psG, T.psL]
        for s, (kk, o, h) in enumerate(jobs):
            g.sync.wait_ge(S["ga%d" % s], 2 if core in loc else 1)
            g.sync.dma_start(T.grow[0:1, 256 * s:256 * s + 256], T.gl[s]).then_inc(S["dg%d" % s], 16)
        for s, (kk, o, h) in enumerate(jobs):
            if s == 0:
                PE.wait_ge(S.wh, 4)
                PE.wait_ge(S.wa, nwa)
                PE.wait_ge(S.v, 1)
            PE.wait_ge(S["ta%d" % s], 4)
            pl, al = [], []
            for f in range(4):
                pl.append(tick("p", PE.matmul(HB[f][:, 0:128], T.W[:, 128 * f:128 * f + 128],
                                              T.tok[:, 128 * s:128 * s + 128], True, True)))
            for f in range(4):
                A.wait_ge(S.p, pl[f])
                al.append(tick("a", A.activation(T.hs[:, 512 * s + 128 * f:512 * s + 128 * f + 128], HB[f][:, 0:128],
                                                 AF.Relu)))
            PE.wait_ge(S["dg%d" % s], 16)
            pg = tick("p", PE.matmul(GBK[s][:, 0:128], T.onesf[0:1, :],
                                     T.grow[0:1, 256 * s + 128 * h:256 * s + 128 * h + 128], True, True))
            for f in range(4):
                PE.wait_ge(S.a, al[f])
                m = PE.matmul(OB[s][:, 0:128], T.W[:, 512 + 128 * f:640 + 128 * f],
                              T.hs[:, 512 * s + 128 * f:512 * s + 128 * f + 128], f == 0, f == 3)
                if f == 3:
                    po = tick("p", m)
            vw("p", pg)
            v1 = tick("v", V.tensor_copy(T.Gb[:, 128 * s:128 * s + 128], GBK[s][:, 0:128]))
            vw("p", po)
            vw("v", v1)
            v2 = tick("v", V.tensor_tensor(T.ro[:, 128 * s:128 * s + 128], OB[s][:, 0:128],
                                           T.Gb[:, 128 * s:128 * s + 128], OP.mult))
            g.wait_ge(S.v, v2)
            c = colour(o, kk)
            send([([T.cores[o]], T.res[:, 256 * c + 128 * h:256 * c + 128 * h + 128],
                   T.ro[:, 128 * s:128 * s + 128], S["ra%d" % c], parts(T.cores[o], 1, 8)[0])])
        if not jobs:
            g.wait_ge(S.wa, nwa)
        for q in ("v", "a", "p", "ls"):
            if n[q]:
                g.wait_ge(S[q], n[q])
        return

    loc, fo, por, plain = P["local"][r], P["foreign"][r], P["porters"][r], P["plain"][r]
    own = lambda b: b[:, 16 * r:16 * r + 16]

    g.sync.dma_start(T.pk[:], T.pick[:]).then_inc(S.dp, 16)
    A.dma_start(T.gt[:], T.gate[:]).then_inc(S.dgt, 16)
    g.sync.dma_start(T.W[:, 0:512], T.w1[:]).then_inc(S.dw, 16)
    A.dma_start(T.W[:, 512:1024], T.w2[:]).then_inc(S.dw, 16)
    g.sync.dma_start(T.xs[:, 0:2048], T.x[:, 0:2048]).then_inc(S.dx, 16)

    v_ones = tick("v", V.memset(T.ones[:], 1.0))
    v_nb = tick("v", V.memset(T.nb[:], -16384.0))
    v_pad = tick("v", V.memset(T.xs[:, 2048:2049], 0.0))
    v_onesf = tick("v", V.memset(T.onesf[:], 1.0))
    A.wait_ge(S.v, v_pad)
    A.dma_start(T.xs[:, 2049:4097], T.x[:, 2048:4096]).then_inc(S.dx, 16)
    i_ci = tick("gi", g.iota(T.ci[:], [[1, 16]], 0, 0))
    i_oc = tick("gi", g.iota(T.oc[:], [[0, 9], [1, 16]], 0, 0, allow_small_or_imprecise_dtypes=True))
    g.wait_ge(S.v, v_nb)
    i_U = tick("gi", g.affine_select(T.U[:], T.ones[:], [[1, 128]], OP.is_gt, 0.0, 0, -1))
    i_nI = tick("gi", g.affine_select(T.nI[:], T.nb[:], [[1, 128]], OP.is_equal, 0.0, 0, -1))
    i_rw = tick("gi", g.iota(T.rowc[:], [[0, 9], [256, 16]], 16384, 0, allow_small_or_imprecise_dtypes=True))
    i_m = tick("gi", g.iota(T.m16[:], [[0, 8], [1, 16]], 0, 0, allow_small_or_imprecise_dtypes=True))
    i_st = tick("gi", g.iota(T.st16[:], [[16, 144]], 0, 0, allow_small_or_imprecise_dtypes=True))
    i_pi = tick("gi", g.iota(T.pi[:], [[0, 1]], 0, 1))
    vw("gi", i_oc)
    v_ci = tick("v", V.tensor_copy(T.cidx[:], T.ci[:]))
    v_rm = tick("v", V.tensor_scalar(T.rm[:], T.oc[:], 0.0, 100000.0, OP.is_equal, OP.mult))

    g.wait_ge(S.dw, 32)
    ms = parts(por[0], 3, 4)
    send([([c], T.W[:, 256 * i:256 * i + 256], T.W[:, 256 * i:256 * i + 256], S.wh, ms[i]) for i, c in enumerate(por)])
    ms = parts(fo[0], 2, 4)
    send([([fo[6 + j]], T.W[:, 768 + 128 * j:896 + 128 * j], T.W[:, 768 + 128 * j:896 + 128 * j], S.wh, ms[j])
          for j in (0, 1)])
    ms = parts(plain[0], 4, 4)
    send([([c], T.W[:, 768 + 64 * i:832 + 64 * i], T.W[:, 768 + 64 * i:832 + 64 * i], S.wh, ms[i])
          for i, c in enumerate(plain)])

    vw("dp", 16)
    v1 = tick("v", V.tensor_scalar(T.ow[:], T.pk[:], 12, None, OP.arith_shift_right))
    v2 = tick("v", V.tensor_scalar(T.loc[:], T.pk[:], TK - 1, None, OP.bitwise_and))
    vw("v", v1)
    v_E = tick("v", V.tensor_tensor(T.E[:], T.ow[:, 0:9].indirect(T.cidx[:, 0:9]), T.oc[:], OP.is_equal))
    vw("v", v2)
    v3 = tick("v", V.tensor_scalar(T.ge[:], T.loc[:], 2048.0, -2048.0, OP.is_ge, OP.add))
    vw("v", v3)
    v_df = tick("v", V.tensor_tensor(T.df[:], T.loc[:], T.ge[:], OP.add))
    PE.wait_ge(S.gi, i_rw)
    PE.wait_ge(S.v, v_E)
    PE.matmul(T.psP[:, 0:144], T.U[:], T.E[:], True, False)
    for s in range(1, 9):
        PE.matmul(T.psP[:, 16 * s:144], T.ones[:], T.E[:, 0:144 - 16 * s], False, False)
    PE.matmul(T.psP[:, 0:144], T.nI[:], T.E[:], False, False)
    p_pos = tick("p", PE.matmul(T.psP[:, 0:144], T.ones[0:1, :], T.rowc[0:1, :], False, True))
    vw("p", p_pos)
    vw("v", v_df)
    v_sc = tick("v", V.tensor_tensor_scan(T.sc[:], T.rm[:], T.psP[:, 0:144], 0.0, OP.max, OP.min))
    vw("v", v_sc)
    v4 = tick("v", V.tensor_scalar(T.cci[:], T.sc[:, 15::16], 0.0625, -0.46875, OP.mult, OP.add))
    vw("v", v4)
    v5 = tick("v", V.tensor_scalar(T.cc16[:], T.cci[:], 16.0, None, OP.mult))
    vw("v", v5)
    vw("gi", i_st)
    for c in range(9):
        sv, cv = T.sc[:, 16 * c + 15:16 * c + 16], T.cc16[:, c:c + 1]
        tick("v", V.tensor_scalar(T.LQ[:, 128 * c:128 * c + 128], T.m16[:], cv, sv, OP.add, OP.is_equal))
        vv = tick("v", V.tensor_scalar(T.RC[:, 144 * c:144 * c + 144], T.st16[:], cv, T.df[:, c:c + 1],
                                       OP.is_equal, OP.mult))
        PE.wait_ge(S.v, vv)
        m = PE.matmul(T.psL[:, 0:144], T.LQ[:, 128 * c:128 * c + 128], T.RC[:, 144 * c:144 * c + 144], c == 0, c == 8)
    p_L = tick("p", m)
    vw("p", p_L)
    v_L = tick("v", V.tensor_scalar(T.L16[:], T.psL[:, 0:144], 2048.0, None, OP.add))

    g.wait_ge(S.v, v_L)
    for i in range(4):
        it = []
        for j in (0, 1):
            c = 2 * i + j
            o = (r - 1 - c) % N
            d = T.cores[o]
            it.append(([d], own(T.Lt), T.L16[:, 16 * o:16 * o + 16], S["l%d" % c], parts(d, 2, 4)[j]))
        send(it)

    vw("dgt", 16)
    for c in range(9):
        sv, cv = T.sc[:, 16 * c + 15:16 * c + 16], T.cc16[:, c:c + 1]
        tick("v", V.tensor_scalar(T.GA[:, 144 * c:144 * c + 144], T.st16[:], cv, T.gt[:, c:c + 1],
                                  OP.is_equal, OP.mult))
        vv = tick("v", V.tensor_scalar(T.GQ[:, 16 * c:16 * c + 16], T.m16[:, 0:16], cv, sv, OP.add, OP.is_equal))
        PE.wait_ge(S.v, vv)
        PE.matmul(T.psG[:, 0:16], T.GA[:, 144 * c:144 * c + 128], T.GQ[:, 16 * c:16 * c + 16], c == 0, c == 8)
        m = PE.matmul(T.psP[0:16, 0:16], T.GA[:, 144 * c + 128:144 * c + 144], T.GQ[:, 16 * c:16 * c + 16],
                      c == 0, c == 8)
    p_G = tick("p", m)

    vw("dx", 32)
    vw("v", v_L)
    v_own = tick("v", V.tensor_copy(T.gx[:, 2048:2304], T.xs[:, 0:4097].indirect(own(T.L16))))
    vw("p", p_G)
    tick("v", V.tensor_copy(T.gs1[:], T.psG[:, 0:16]))
    v_gs = tick("v", V.tensor_copy(T.gs2[0:16, :], T.psP[0:16, 0:16]))
    v_g = []
    for c in range(8):
        k = (r + 1 + c) % N
        vw("l%d" % c, 4)
        v_g.append(tick("v", V.tensor_copy(T.gx[:, 256 * c:256 * c + 256],
                                           T.xs[:, 0:4097].indirect(T.Lt[:, 16 * k:16 * k + 16]))))
    g.sync.wait_ge(S.v, v_gs)
    g.sync.dma_start(T.gd[0:8], T.gs1[:]).then_inc(S.dgs, 16)
    g.sync.dma_start(T.gd[8], T.gs2[0:16, :]).then_inc(S.dgs, 16)
    g.sync.wait_ge(S.dgs, 32)
    g.sync.dma_start(T.grow[0:1, 0:256], T.gd[r]).then_inc(S.dgr, 16)

    used = {}
    for c in range(0, 6, 2):
        g.wait_ge(S.v, v_g[c + 1])
        it = []
        for j in (0, 1):
            d = P["relay"][r][ROLE[c + j]]
            s = used.get(d, 0)
            used[d] = s + 1
            it.append(([d], T.rl[:, 256 * s:256 * s + 256], T.gx[:, 256 * (c + j):256 * (c + j) + 256],
                       S["rl%d" % s], parts(d, 2, 8)[j]))
        send(it)
    g.wait_ge(S.dgs, 32)
    for site, w in ((loc, 2), (fo, 1)):
        it = []
        for c in site:
            for s, (kk, o, h) in enumerate(P["jobs"].get(c, [])):
                it.append(([c], T.gl[s], T.gd[o], S["ga%d" % s], parts(c, 8, w)[len(it)]))
        send(it)
    for c in (6, 7):
        g.wait_ge(S.v, v_g[c])
        dispatch((r + 1 + c) % N, r, T.gx, 256 * c)

    A.wait_ge(S.dx, 32)
    A.wait_ge(S.v, v_pad)
    tick("a", A.activation(T.yb[:, 0:4097], T.xs[:, 0:4097], AF.Copy, scale=0.0))
    a_y = tick("a", A.activation(T.yb[:, 4097:4353], T.xs[:, 0:256], AF.Copy, scale=0.0))

    PE.wait_ge(S.dw, 32)
    PE.wait_ge(S.v, v_own)
    pl, al = [], []
    for f in range(4):
        pl.append(tick("p", PE.matmul(HB[f][:, 0:256], T.W[:, 128 * f:128 * f + 128], T.gx[:, 2048:2304], True, True)))
    for f in range(4):
        A.wait_ge(S.p, pl[f])
        al.append(tick("a", A.activation(T.hs[:, 256 * f:256 * f + 256], HB[f][:, 0:256], AF.Relu)))
    for f in range(4):
        PE.wait_ge(S.a, al[f])
        m = PE.matmul(T.po[:, 0:256], T.W[:, 512 + 128 * f:640 + 128 * f], T.hs[:, 256 * f:256 * f + 256],
                      f == 0, f == 3)
    p_o = tick("p", m)
    PE.wait_ge(S.dgr, 16)
    p_gb = tick("p", PE.matmul(T.psL[:, 0:256], T.onesf[0:1, :], T.grow[0:1, 0:256], True, True))

    vw("gi", i_pi)
    vc = tick("v", V.tensor_copy(own(T.Lt), own(T.L16)))
    v1 = tick("v", V.tensor_scalar(T.pm[:], T.pi[:], 15, None, OP.bitwise_and))
    vw("v", v1)
    v1 = tick("v", V.tensor_scalar(T.pf[:], T.pm[:], 2049.0, None, OP.add))
    v2 = tick("v", V.tensor_copy(T.lf[:], T.Lt[:]))
    vw("v", v2)
    v3 = tick("v", V.tensor_scalar(T.ub[:], T.oc[:], 16.0, T.pf[:], OP.mult, OP.add))
    v4 = tick("v", V.tensor_scalar(T.lm[:], T.lf[:], 2048.0, None, OP.is_equal))
    vw("v", v4)
    v5 = tick("v", V.tensor_tensor(T.lm[:], T.lm[:], T.ub[:], OP.mult))
    vw("v", v5)
    v6 = tick("v", V.tensor_tensor(T.lf[:], T.lf[:], T.lm[:], OP.add))
    vw("v", v6)
    v7 = tick("v", V.tensor_copy(T.L2[:], T.lf[:]))

    vw("p", p_gb)
    v8 = tick("v", V.tensor_copy(T.Gb[:], T.psL[:, 0:256]))
    vw("v", v8)
    v9 = tick("v", V.tensor_tensor(T.ro[:], T.po[:, 0:256], T.Gb[:], OP.mult))
    vw("v", v9)
    vw("a", a_y)
    vs = tick("v", V.tensor_copy(T.yb[:, 0:4353].indirect(own(T.L2)), T.ro[:]))
    for c in range(8):
        k = (r + 1 + c) % N
        L = T.L2[:, 16 * k:16 * k + 16]
        t = T.tmp[:, 256 * (c % 2):256 * (c % 2) + 256]
        vw("ra%d" % c, 16)
        vw("v", vs)
        va = tick("v", V.tensor_tensor(t, T.yb[:, 0:4353].indirect(L), T.res[:, 256 * c:256 * c + 256], OP.add))
        vw("v", va)
        vs = tick("v", V.tensor_copy(T.yb[:, 0:4353].indirect(L), t))
    g.sync.wait_ge(S.v, vs)
    g.sync.dma_start(T.y[:, 0:2048], T.yb[:, 0:2048]).then_inc(S.dy, 16)
    A.wait_ge(S.v, vs)
    A.dma_start(T.y[:, 2048:4096], T.yb[:, 2049:4097]).then_inc(S.dy, 16)
    for q in ("gi", "v", "a", "p", "ls"):
        g.wait_ge(S[q], n[q])
    g.wait_ge(S.dy, 32)
